import numpy as np
import ml_dtypes


def mxq(x, axis, fmt="e4m3"):
    dtype, down = {"e4m3": (ml_dtypes.float8_e4m3fn, 7), "e5m2": (ml_dtypes.float8_e5m2, 14)}[fmt]
    v = np.moveaxis(np.asarray(x, np.float32).astype(ml_dtypes.bfloat16).astype(np.float64), axis, -1)
    blocks = v.reshape(v.shape[:-1] + (-1, 32))
    amax = np.abs(blocks).max(-1, keepdims=True)
    byte = np.maximum(np.where(amax > 0, np.frexp(amax)[1] - 1 + 127, 0) - down, 1)
    scale = np.exp2(byte - 127.0)
    codes = (blocks / scale).astype(np.float32).astype(dtype).astype(np.float64)
    return np.moveaxis((codes * scale).reshape(v.shape), -1, axis)


WIDE = False


def mx_kscale(k):
    if not WIDE:
        return np.ones(k)
    levels = np.array([10, -10, 5, -5, 0])
    if k % 512:
        return np.exp2(np.random.permutation(np.resize(levels, k // 32))).repeat(32)
    a = np.empty((k // 512, 16))
    for p in range(k // 512):
        a[p, :8] = np.random.permutation(np.resize(levels, 8))
        for g in range(8):
            far = levels[np.abs(levels - a[p, g]) >= 10]
            a[p, g + 8] = far[np.random.randint(len(far))]
    return np.exp2(a.ravel()).repeat(32)


def f64(x):
    return np.asarray(x).astype(np.float64)


def striped(idx):
    return np.tile(idx.reshape(-1, 16).T, (8, 1)).astype(np.uint16)


def unstriped(offs):
    return offs[:16].T.reshape(-1).astype(np.int64)


def striped8(idx):
    return np.concatenate([x.reshape(-1, 16).T for x in idx]).astype(np.uint16)


def runs(offs, k):
    lists = np.stack([offs[16 * r : 16 * r + 16].T.reshape(-1) for r in range(8)]).astype(np.int64)
    return lists[np.arange(k) % 512 // 64]


def pack_weight(w):
    k, n = w.shape
    w = f64(np.asarray(w, np.float32).astype(ml_dtypes.bfloat16)).reshape(k // 32, 32, n)
    amax = np.abs(w).max(1)
    byte = np.clip(np.where(amax > 0, np.frexp(amax)[1] - 1 + 127 - 7, 1), 1, 254)
    scaled = (w * np.exp2(127.0 - byte)[:, None, :]).reshape(k, n).astype(np.float32)
    words = np.ascontiguousarray(scaled.reshape(k // 512, 128, 4, n).transpose(0, 1, 3, 2)).astype(ml_dtypes.float8_e4m3fn).view(np.uint8)
    return words, np.ascontiguousarray(byte.astype(np.uint8).reshape(k // 512, 16, n))


def unpack_weight(words, scales):
    g, p, n, _ = words.shape
    vals = np.ascontiguousarray(words).view(ml_dtypes.float8_e4m3fn).astype(np.float64) * np.repeat(np.exp2(scales.astype(np.float64) - 127.0), 8, axis=1)[..., None]
    return vals.transpose(0, 1, 3, 2).reshape(g * 512, n)


def sigmoid(v):
    return 1.0 / (1.0 + np.exp(-np.maximum(v, -700.0)))

def planes(y):
    n, m = y.shape
    v = y.astype(np.float32).astype(ml_dtypes.bfloat16).astype(np.float64).reshape(n // 32, 32, m)
    top = np.abs(v).max(1)
    byte = np.clip(np.where(top > 0, np.frexp(top)[1] - 1 + 127 - 7, 1), 1, 254)
    codes = (v * np.exp2(127.0 - byte)[:, None, :]).reshape(n, m).astype(np.float32).astype(ml_dtypes.float8_e4m3fn).view(np.uint8)
    words = codes.reshape(n // 512, 128, 4, m).transpose(0, 1, 3, 2)
    return np.ascontiguousarray(words), np.ascontiguousarray(byte.astype(np.uint8).reshape(n // 512, 16, m))


K, T, S, V, N, U, H = 512, 2048, 512, 512, 512, 1024, 512


def setup_inputs():
    n = np.random.standard_normal
    s = mx_kscale(K)[:, None]
    u = mx_kscale(S)
    packed_xT = pack_weight(n((K, T)) * s)
    packed_w1 = pack_weight(n((K, H)) / np.sqrt(K) / s)
    packed_w2 = pack_weight(n((V, N)) / np.sqrt(V) / u[:, None])
    return {
        "x_words": packed_xT[0],
        "x_scales": packed_xT[1],
        "w1_words": packed_w1[0],
        "w1_scales": packed_w1[1],
        "gs": (np.random.uniform(0.5, 1.5, (K, 1)) / s).astype(np.float32),
        "gt": (np.random.uniform(0.5, 1.5, (V, 1)) * u[:, None]).astype(np.float32),
        "w2_words": packed_w2[0],
        "w2_scales": packed_w2[1],
        "offs": striped(np.random.permutation(T)[:S]),
        "cand": striped(np.random.permutation(T)[:V]),
        "slot": striped8(np.stack([np.random.permutation(U)[:S] for _ in range(8)])),
    }


def reference(x_words, x_scales, w1_words, w1_scales, gs, gt, w2_words, w2_scales, offs, cand, slot):
    x_cand = unpack_weight(x_words, x_scales)[:, unstriped(cand)]
    xq = unpack_weight(x_words, x_scales)[:, unstriped(offs)]
    h = unpack_weight(w1_words, w1_scales).T @ xq
    z = f64(gs) * h
    s = sigmoid(0.0625 * ((x_cand.T @ mxq(z, 0, "e4m3"))))
    pt = np.zeros((V, U))
    pt[np.arange(V)[:, None], runs(slot, V)] = s
    z2 = f64(gt) * pt
    out_0 = unpack_weight(w2_words, w2_scales).T @ mxq(z2, 0, "e4m3")
    return (out_0,) + planes(out_0)

@@ -1,0 +1,234 @@
+from contextlib import ExitStack
+
+import concourse.mybir as mybir
+
+F32 = mybir.dt.float32
+BF16 = mybir.dt.bfloat16
+I32 = mybir.dt.int32
+U32 = mybir.dt.uint32
+U16 = mybir.dt.uint16
+U8 = mybir.dt.uint8
+FP8X4 = mybir.dt.float8_e4m3fn_x4
+ACT = mybir.ActivationFunctionType
+
+P = 128
+PACK = 4
+K, T, S, V, N, U, H = 512, 2048, 512, 512, 512, 1024, 512
+FLOPS = 2 * K * H * S + 2 * K * V * S + 2 * V * N * U
+
+PLACE_SLICES = (256, 256)
+SLOT_CHUNKS = (128, 256, 256, 256, 128)
+
+
+def pieces(start, width):
+    out = []
+    while width > 0:
+        n = 512 if width >= 512 else (256 if width >= 256 else 128)
+        out.append((start, n))
+        start, width = start + n, width - n
+    return out
+
+
+def as_words(packed):
+    return packed[0].rearrange("p n t -> p (n t)").bitcast(I32)
+
+
+def load_scales(queue, plane, scales):
+    for q in range(4):
+        queue.dma_start(out=plane[32 * q : 32 * q + 4, :].bitcast(I32), in_=scales[0, 4 * q : 4 * q + 4, :].bitcast(I32))
+
+
+def load_scales_everywhere(queue, plane, scales):
+    for q in range(4):
+        rows = scales[0, 4 * q : 4 * q + 4, :].bitcast(I32).partition_broadcast(8)
+        queue.dma_start(out=plane[32 * q : 32 * q + 32, :].bitcast(I32), in_=rows)
+
+
+def dealt(tile):
+    return tile[:].rearrange("p (t m) -> p m t", t=PACK)
+
+
+def in_fours(tile):
+    return tile[:].rearrange("p (m t) -> p m t", t=PACK)
+
+
+def join_pairs(nc, grouped, pairs):
+    nc.vector.tensor_copy(
+        out=grouped[:].bitcast(I32).rearrange("p (n u) -> p n u", u=2),
+        in_=pairs[:].bitcast(I32).rearrange("p (u n) -> p n u", u=2),
+    )
+
+
+def pair_slot(pairs, t):
+    return pairs[:].rearrange("p (u n e) -> p u n e", u=2, e=2)[:, t // 2, :, t % 2]
+
+
+def tile_picked_candpage_sigmoid_po_kernel(
+    tc, x_words, x_scales, w1_words, w1_scales, gs, gt, w2_words, w2_scales, offs, cand, slot, out_0, out_1, out_2
+):
+    nc = tc.nc
+    with ExitStack() as ctx:
+        keep = ctx.enter_context(tc.tile_pool(name="keep", bufs=1))
+        psum = ctx.enter_context(tc.psum_pool(name="psum", bufs=8))
+
+        def sbuf(name, shape, dtype):
+            return keep.tile(shape, dtype, name=name, align_bytes=64)
+
+        def bank(shape):
+            return psum.tile(shape, F32, name="bank")
+
+        def mx(out, lhs, lhs_cols, rhs, rhs_cols):
+            nc.tensor.matmul_mx(
+                out=out,
+                lhsT=lhs[0][:, lhs_cols].bitcast(FP8X4),
+                lhsT_scale=lhs[1][:, lhs_cols],
+                rhs=rhs[0][:, rhs_cols].bitcast(FP8X4),
+                rhs_scale=rhs[1][:, rhs_cols],
+                start=True,
+                stop=True,
+            )
+
+        offs_t = keep.tile([P, S // 16], U16, name="offs_t")
+        cand_t = keep.tile([P, V // 16], U16, name="cand_t")
+        slot_t = keep.tile([P, S // 16], U16, name="slot_t")
+        x_w = sbuf("x_w", [P, T], U32)
+        x_s = sbuf("x_s", [P, T], U8)
+        w1_raw = (sbuf("w_raw_w", [P, H], U32), sbuf("w_raw_s", [P, H], U8))
+        gs_t = sbuf("gs_t", [P, PACK], F32)
+        gt_t = sbuf("gt_t", [P, PACK], F32)
+        windows = [sbuf(f"window{t}", [P, U], F32) for t in range(PACK)]
+
+        for t in range(PACK):
+            nc.vector.memset(windows[t][:], 0.0)
+        nc.vector.memset(w1_raw[1][:].bitcast(I32), 0)
+
+        nc.sync.dma_start(offs_t[:], offs)
+        load_scales_everywhere(nc.sync, x_s, x_scales)
+        nc.sync.dma_start(out=w1_raw[0][:].bitcast(I32), in_=as_words(w1_words))
+        nc.sync.dma_start(cand_t[:], cand)
+        nc.sync.dma_start(out=x_w[:].bitcast(I32), in_=as_words(x_words))
+        nc.sync.dma_start(out=gs_t[:], in_=gs.rearrange("(p t) o -> p (t o)", t=PACK))
+        nc.sync.dma_start(slot_t[:], slot)
+        nc.sync.dma_start(out=gt_t[:], in_=gt.rearrange("(p t) o -> p (t o)", t=PACK))
+        load_scales(nc.sync, w1_raw[1], w1_scales)
+
+        xq_s = sbuf("xq_s", [P, S], U8)
+        xc = (sbuf("xc_w", [P, V], U32), sbuf("xc_s", [P, V], U8))
+        w1 = (sbuf("w1_w", [P, H], U32), sbuf("w1_s", [P, H], U8))
+        w2 = (sbuf("w2_w", [P, N], U32), sbuf("w2_s", [P, N], U8))
+        zq = (sbuf("z_w", [P, S], U32), sbuf("z_s", [P, S], U8))
+
+        nc.vector.tensor_copy(out=xq_s[:], in_=x_s[:].indirect(offs_t[:]))
+        nc.vector.tensor_copy(out=dealt(xc[1]), in_=x_s[:].indirect(cand_t[:]))
+        nc.scalar.copy(out=dealt(w1[0]), in_=in_fours(w1_raw[0]))
+        nc.vector.tensor_copy(out=dealt(w1[1]), in_=in_fours(w1_raw[1]))
+
+        w2_raw = (sbuf("w_raw_w", [P, N], U32), sbuf("w_raw_s", [P, N], U8))
+        nc.vector.memset(w2_raw[1][:].bitcast(I32), 0)
+        nc.sync.dma_start(out=w2_raw[0][:].bitcast(I32), in_=as_words(w2_words))
+        load_scales(nc.sync, w2_raw[1], w2_scales)
+
+        def gather_places(j0, n, name):
+            words = sbuf(name, [P, n], U32)
+            nc.vector.tensor_copy(out=words[:], in_=x_w[:].indirect(offs_t[:, j0 // 16 : (j0 + n) // 16]))
+            return words
+
+        def project(j0, n, words, on_vector):
+            pairs = sbuf(f"z_pairs{j0}", [P, PACK * n], BF16)
+            for u in range(2):
+                h = bank([P, 2, n])
+                for e in range(2):
+                    t = 2 * u + e
+                    mx(h[:, e, :], w1, slice(P * t, P * t + P), (words, xq_s[:, j0 : j0 + n]), slice(0, n))
+                if u in on_vector:
+                    nc.vector.tensor_tensor(
+                        out=pairs[:, 2 * n * u : 2 * n * (u + 1)].rearrange("p (n e) -> p n e", e=2),
+                        in0=h[:].rearrange("p e n -> p n e"),
+                        in1=gs_t[:, 2 * u : 2 * u + 2].unsqueeze(1).to_broadcast([P, n, 2]),
+                        op=mybir.AluOpType.mult,
+                    )
+                else:
+                    for e in range(2):
+                        t = 2 * u + e
+                        nc.scalar.activation(
+                            out=pair_slot(pairs, t), in_=h[:, e, :], func=ACT.Copy, scale=gs_t[:, t : t + 1]
+                        )
+            return pairs
+
+        def join_z(n, pairs, name):
+            grouped = sbuf(name, [P, PACK * n], BF16)
+            join_pairs(nc, grouped, pairs)
+            return grouped
+
+        def quantise_z(j0, n, grouped):
+            nc.vector.quantize_mx(out=zq[0][:, j0 : j0 + n].bitcast(FP8X4), scales=zq[1][:, j0 : j0 + n], in_=grouped[:])
+
+        def score_and_scatter(t, j0, n):
+            logits = bank([P, n])
+            mx(logits[:], xc, slice(P * t, P * t + P), zq, slice(j0, j0 + n))
+            scores = sbuf(f"scores{t}_{j0}", [P, n], F32)
+            nc.scalar.activation(out=scores[:], in_=logits[:], func=ACT.Sigmoid, scale=0.0625)
+            target = windows[t][:].indirect(slot_t[:, j0 // 16 : (j0 + n) // 16])
+            nc.vector.tensor_copy(out=target, in_=scores[:])
+
+        chunks = []
+        w0 = 0
+        for width in SLOT_CHUNKS:
+            chunks.append((w0, width, sbuf(f"z2_pairs{w0}", [P, PACK * width], BF16)))
+            w0 += width
+
+        def weigh(t, chunk):
+            w0, width, pairs = chunk
+            nc.scalar.activation(
+                out=pair_slot(pairs, t), in_=windows[t][:, w0 : w0 + width], func=ACT.Copy, scale=gt_t[:, t : t + 1]
+            )
+
+        first, rest = PLACE_SLICES
+        words = gather_places(0, first, "xq_first")
+        nc.vector.tensor_copy(out=dealt(xc[0]), in_=x_w[:].indirect(cand_t[:]))
+        quantise_z(0, first, join_z(first, project(0, first, words, (1,)), "shared"))
+        words = gather_places(first, rest, "shared")
+        score_and_scatter(0, 0, first)
+        score_and_scatter(1, 0, first)
+        grouped = join_z(rest, project(first, rest, words, ()), "z_grouped_rest")
+        score_and_scatter(2, 0, first)
+        quantise_z(first, rest, grouped)
+        score_and_scatter(3, 0, first)
+        nc.scalar.copy(out=dealt(w2[0]), in_=in_fours(w2_raw[0]))
+        nc.vector.tensor_copy(out=dealt(w2[1]), in_=in_fours(w2_raw[1]))
+        for t in range(PACK):
+            score_and_scatter(t, first, rest)
+        for t in range(PACK):
+            for chunk in chunks:
+                weigh(t, chunk)
+
+        z2q = (sbuf("z2_w", [P, U], U32), sbuf("z2_s", [P, U], U8))
+        yq = (sbuf("y_w", [P, U], U32), sbuf("y_s", [P, U], U8))
+        out_rows = out_0.rearrange("(p t) w -> p t w", t=PACK)
+        out_words = as_words(out_1)
+        for w0, width, pairs in chunks:
+            cols = slice(w0, w0 + width)
+            grouped = sbuf(f"z2_grouped{w0}", [P, PACK * width], BF16)
+            join_pairs(nc, grouped, pairs)
+            nc.vector.quantize_mx(out=z2q[0][:, cols].bitcast(FP8X4), scales=z2q[1][:, cols], in_=grouped[:])
+        for w0, width, pairs in chunks:
+            cols = slice(w0, w0 + width)
+            y = sbuf(f"y{w0}", [P, PACK, width], F32)
+            per_bank = 512 // width
+            for t0 in range(0, PACK, per_bank):
+                acc = bank([P, per_bank, width])
+                for i in range(per_bank):
+                    t = t0 + i
+                    mx(acc[:, i, :], w2, slice(P * t, P * t + P), z2q, cols)
+                nc.scalar.copy(out=y[:, t0 : t0 + per_bank, :], in_=acc[:])
+                nc.sync.dma_start(out=out_rows[:, t0 : t0 + per_bank, cols], in_=y[:, t0 : t0 + per_bank, :])
+            y_grouped = sbuf(f"y_grouped{w0}", [P, PACK * width], BF16)
+            nc.vector.tensor_copy(
+                out=y_grouped[:].rearrange("p (c i t) -> p c t i", i=4, t=PACK),
+                in_=y[:].rearrange("p t (c i) -> p c t i", i=4),
+            )
+            nc.vector.quantize_mx(out=yq[0][:, cols].bitcast(FP8X4), scales=yq[1][:, cols], in_=y_grouped[:])
+            nc.sync.dma_start(out=out_words[:, cols], in_=yq[0][:, cols].bitcast(I32))
+        for q in range(4):
+            queue = nc.sync if q % 2 == 0 else nc.scalar
+            queue.dma_start(out=out_2[0, 4 * q : 4 * q + 4, :].bitcast(I32), in_=yq[1][32 * q : 32 * q + 4, :].bitcast(I32))

@@ -16,8 +16,10 @@ PACK = 4
 K, T, S, V, N, U, H = 512, 2048, 512, 512, 512, 1024, 512
 FLOPS = 2 * K * H * S + 2 * K * V * S + 2 * V * N * U
 
-PLACE_SLICES = (256, 256)
+PLACE_SLICES = (128, 384)
+Z2_CHUNKS = (128, 256, 256, 384)
 SLOT_CHUNKS = (128, 256, 256, 256, 128)
+WORD_STORE_ENDS = (384, 896, 1024)
 
 
 def pieces(start, width):
@@ -93,66 +95,53 @@ def tile_picked_candpage_sigmoid_po_kernel(
         slot_t = keep.tile([P, S // 16], U16, name="slot_t")
         x_w = sbuf("x_w", [P, T], U32)
         x_s = sbuf("x_s", [P, T], U8)
-        w1_raw = (sbuf("w_raw_w", [P, H], U32), sbuf("w_raw_s", [P, H], U8))
+        w1_raw = (sbuf("w_raw_w", [P, H], U32), sbuf("w1_raw_s", [P, H], U8))
         gs_t = sbuf("gs_t", [P, PACK], F32)
         gt_t = sbuf("gt_t", [P, PACK], F32)
         windows = [sbuf(f"window{t}", [P, U], F32) for t in range(PACK)]
 
-        for t in range(PACK):
-            nc.vector.memset(windows[t][:], 0.0)
         nc.vector.memset(w1_raw[1][:].bitcast(I32), 0)
+        for t in range(PACK):
+            engine = nc.vector if t < 2 else nc.gpsimd
+            engine.memset(windows[t][:], 0.0)
 
         nc.sync.dma_start(offs_t[:], offs)
         load_scales_everywhere(nc.sync, x_s, x_scales)
-        nc.sync.dma_start(out=w1_raw[0][:].bitcast(I32), in_=as_words(w1_words))
         nc.sync.dma_start(cand_t[:], cand)
         nc.sync.dma_start(out=x_w[:].bitcast(I32), in_=as_words(x_words))
-        nc.sync.dma_start(out=gs_t[:], in_=gs.rearrange("(p t) o -> p (t o)", t=PACK))
-        nc.sync.dma_start(slot_t[:], slot)
-        nc.sync.dma_start(out=gt_t[:], in_=gt.rearrange("(p t) o -> p (t o)", t=PACK))
+        nc.sync.dma_start(out=w1_raw[0][:].bitcast(I32), in_=as_words(w1_words))
         load_scales(nc.sync, w1_raw[1], w1_scales)
+        nc.sync.dma_start(slot_t[:], slot)
+        nc.gpsimd.dma_start(out=gs_t[:], in_=gs.rearrange("(p t) o -> p (t o)", t=PACK))
+        nc.gpsimd.dma_start(out=gt_t[:], in_=gt.rearrange("(p t) o -> p (t o)", t=PACK))
 
         xq_s = sbuf("xq_s", [P, S], U8)
-        xc = (sbuf("xc_w", [P, V], U32), sbuf("xc_s", [P, V], U8))
+        xc_s = sbuf("xc_s", [P, V], U8)
         w1 = (sbuf("w1_w", [P, H], U32), sbuf("w1_s", [P, H], U8))
-        w2 = (sbuf("w2_w", [P, N], U32), sbuf("w2_s", [P, N], U8))
         zq = (sbuf("z_w", [P, S], U32), sbuf("z_s", [P, S], U8))
 
         nc.vector.tensor_copy(out=xq_s[:], in_=x_s[:].indirect(offs_t[:]))
-        nc.vector.tensor_copy(out=dealt(xc[1]), in_=x_s[:].indirect(cand_t[:]))
+        nc.vector.tensor_copy(out=dealt(xc_s), in_=x_s[:].indirect(cand_t[:]))
         nc.scalar.copy(out=dealt(w1[0]), in_=in_fours(w1_raw[0]))
         nc.vector.tensor_copy(out=dealt(w1[1]), in_=in_fours(w1_raw[1]))
 
-        w2_raw = (sbuf("w_raw_w", [P, N], U32), sbuf("w_raw_s", [P, N], U8))
-        nc.vector.memset(w2_raw[1][:].bitcast(I32), 0)
-        nc.sync.dma_start(out=w2_raw[0][:].bitcast(I32), in_=as_words(w2_words))
-        load_scales(nc.sync, w2_raw[1], w2_scales)
+        w2_raw_s = sbuf("x_s", [P, N], U8)
+        nc.vector.memset(w2_raw_s[:].bitcast(I32), 0)
+        load_scales(nc.sync, w2_raw_s, w2_scales)
 
         def gather_places(j0, n, name):
             words = sbuf(name, [P, n], U32)
             nc.vector.tensor_copy(out=words[:], in_=x_w[:].indirect(offs_t[:, j0 // 16 : (j0 + n) // 16]))
             return words
 
-        def project(j0, n, words, on_vector):
+        def project(j0, n, words):
             pairs = sbuf(f"z_pairs{j0}", [P, PACK * n], BF16)
-            for u in range(2):
-                h = bank([P, 2, n])
-                for e in range(2):
-                    t = 2 * u + e
-                    mx(h[:, e, :], w1, slice(P * t, P * t + P), (words, xq_s[:, j0 : j0 + n]), slice(0, n))
-                if u in on_vector:
-                    nc.vector.tensor_tensor(
-                        out=pairs[:, 2 * n * u : 2 * n * (u + 1)].rearrange("p (n e) -> p n e", e=2),
-                        in0=h[:].rearrange("p e n -> p n e"),
-                        in1=gs_t[:, 2 * u : 2 * u + 2].unsqueeze(1).to_broadcast([P, n, 2]),
-                        op=mybir.AluOpType.mult,
-                    )
-                else:
-                    for e in range(2):
-                        t = 2 * u + e
-                        nc.scalar.activation(
-                            out=pair_slot(pairs, t), in_=h[:, e, :], func=ACT.Copy, scale=gs_t[:, t : t + 1]
-                        )
+            for t in range(PACK):
+                h = bank([P, n])
+                for a, width in pieces(0, n):
+                    cols = slice(a, a + width)
+                    mx(h[:, cols], w1, slice(P * t, P * t + P), (words, xq_s[:, j0 : j0 + n]), cols)
+                nc.scalar.activation(out=pair_slot(pairs, t), in_=h[:], func=ACT.Copy, scale=gs_t[:, t : t + 1])
             return pairs
 
         def join_z(n, pairs, name):
@@ -163,18 +152,40 @@ def tile_picked_candpage_sigmoid_po_kernel(
         def quantise_z(j0, n, grouped):
             nc.vector.quantize_mx(out=zq[0][:, j0 : j0 + n].bitcast(FP8X4), scales=zq[1][:, j0 : j0 + n], in_=grouped[:])
 
-        def score_and_scatter(t, j0, n):
+        def score_and_scatter(t, j0, n, name=None):
             logits = bank([P, n])
-            mx(logits[:], xc, slice(P * t, P * t + P), zq, slice(j0, j0 + n))
-            scores = sbuf(f"scores{t}_{j0}", [P, n], F32)
+            for a, width in pieces(0, n):
+                mx(logits[:, a : a + width], xc, slice(P * t, P * t + P), zq, slice(j0 + a, j0 + a + width))
+            scores = sbuf(name or f"scores{t}_{j0}", [P, n], F32)
             nc.scalar.activation(out=scores[:], in_=logits[:], func=ACT.Sigmoid, scale=0.0625)
             target = windows[t][:].indirect(slot_t[:, j0 // 16 : (j0 + n) // 16])
             nc.vector.tensor_copy(out=target, in_=scores[:])
 
+        first, rest = PLACE_SLICES
+        words_first = gather_places(0, first, "xq_first")
+        words_rest = gather_places(first, rest, "w1_raw_s")
+        pairs_first = project(0, first, words_first)
+        xc = (sbuf("xq_first", [P, V], U32), xc_s)
+        nc.vector.tensor_copy(out=dealt(xc[0]), in_=x_w[:].indirect(cand_t[:]))
+        quantise_z(0, first, join_z(first, pairs_first, "z_grouped_first"))
+        w2_raw_w = sbuf("w_raw_w", [P, N], U32)
+        nc.sync.dma_start(out=w2_raw_w[:].bitcast(I32), in_=as_words(w2_words))
+        score_and_scatter(0, 0, first)
+        quantise_z(first, rest, join_z(rest, project(first, rest, words_rest), "z_grouped_rest"))
+        score_and_scatter(1, 0, first, f"z_pairs{first}")
+        score_and_scatter(2, 0, first)
+        score_and_scatter(3, 0, first, "z_grouped_rest")
+        for t in range(PACK):
+            score_and_scatter(t, first, rest)
+
+        w2 = (sbuf("w1_raw_s", [P, N], U32), sbuf("z_grouped_first", [P, N], U8))
+        w2_raw = (w2_raw_w, w2_raw_s)
+        nc.vector.tensor_copy(out=dealt(w2[1]), in_=in_fours(w2_raw[1]))
+
         chunks = []
         w0 = 0
-        for width in SLOT_CHUNKS:
-            chunks.append((w0, width, sbuf(f"z2_pairs{w0}", [P, PACK * width], BF16)))
+        for width, host in zip(Z2_CHUNKS, ("xq_first", "xc_s", "z_w", "z_s")):
+            chunks.append((w0, width, sbuf(host, [P, PACK * width], BF16)))
             w0 += width
 
         def weigh(t, chunk):
@@ -183,21 +194,7 @@ def tile_picked_candpage_sigmoid_po_kernel(
                 out=pair_slot(pairs, t), in_=windows[t][:, w0 : w0 + width], func=ACT.Copy, scale=gt_t[:, t : t + 1]
             )
 
-        first, rest = PLACE_SLICES
-        words = gather_places(0, first, "xq_first")
-        nc.vector.tensor_copy(out=dealt(xc[0]), in_=x_w[:].indirect(cand_t[:]))
-        quantise_z(0, first, join_z(first, project(0, first, words, (1,)), "shared"))
-        words = gather_places(first, rest, "shared")
-        score_and_scatter(0, 0, first)
-        score_and_scatter(1, 0, first)
-        grouped = join_z(rest, project(first, rest, words, ()), "z_grouped_rest")
-        score_and_scatter(2, 0, first)
-        quantise_z(first, rest, grouped)
-        score_and_scatter(3, 0, first)
         nc.scalar.copy(out=dealt(w2[0]), in_=in_fours(w2_raw[0]))
-        nc.vector.tensor_copy(out=dealt(w2[1]), in_=in_fours(w2_raw[1]))
-        for t in range(PACK):
-            score_and_scatter(t, first, rest)
         for t in range(PACK):
             for chunk in chunks:
                 weigh(t, chunk)
@@ -206,12 +203,13 @@ def tile_picked_candpage_sigmoid_po_kernel(
         yq = (sbuf("y_w", [P, U], U32), sbuf("y_s", [P, U], U8))
         out_rows = out_0.rearrange("(p t) w -> p t w", t=PACK)
         out_words = as_words(out_1)
+        stored = 0
         for w0, width, pairs in chunks:
             cols = slice(w0, w0 + width)
             grouped = sbuf(f"z2_grouped{w0}", [P, PACK * width], BF16)
             join_pairs(nc, grouped, pairs)
             nc.vector.quantize_mx(out=z2q[0][:, cols].bitcast(FP8X4), scales=z2q[1][:, cols], in_=grouped[:])
-        for w0, width, pairs in chunks:
+        for w0, width in zip([sum(SLOT_CHUNKS[:i]) for i in range(len(SLOT_CHUNKS))], SLOT_CHUNKS):
             cols = slice(w0, w0 + width)
             y = sbuf(f"y{w0}", [P, PACK, width], F32)
             per_bank = 512 // width
@@ -221,14 +219,16 @@ def tile_picked_candpage_sigmoid_po_kernel(
                     t = t0 + i
                     mx(acc[:, i, :], w2, slice(P * t, P * t + P), z2q, cols)
                 nc.scalar.copy(out=y[:, t0 : t0 + per_bank, :], in_=acc[:])
-                nc.sync.dma_start(out=out_rows[:, t0 : t0 + per_bank, cols], in_=y[:, t0 : t0 + per_bank, :])
+            nc.sync.dma_start(out=out_rows[:, :, cols], in_=y[:])
             y_grouped = sbuf(f"y_grouped{w0}", [P, PACK * width], BF16)
             nc.vector.tensor_copy(
                 out=y_grouped[:].rearrange("p (c i t) -> p c t i", i=4, t=PACK),
                 in_=y[:].rearrange("p t (c i) -> p c t i", i=4),
             )
             nc.vector.quantize_mx(out=yq[0][:, cols].bitcast(FP8X4), scales=yq[1][:, cols], in_=y_grouped[:])
-            nc.sync.dma_start(out=out_words[:, cols], in_=yq[0][:, cols].bitcast(I32))
+            if w0 + width in WORD_STORE_ENDS:
+                nc.sync.dma_start(out=out_words[:, stored : w0 + width], in_=yq[0][:, stored : w0 + width].bitcast(I32))
+                stored = w0 + width
         for q in range(4):
             queue = nc.sync if q % 2 == 0 else nc.scalar
             queue.dma_start(out=out_2[0, 4 * q : 4 * q + 4, :].bitcast(I32), in_=yq[1][32 * q : 32 * q + 4, :].bitcast(I32))

@@ -97,13 +97,11 @@ def tile_picked_candpage_sigmoid_po_kernel(
         x_s = sbuf("x_s", [P, T], U8)
         w1_raw = (sbuf("w_raw_w", [P, H], U32), sbuf("w1_raw_s", [P, H], U8))
         gs_t = sbuf("gs_t", [P, PACK], F32)
-        gt_t = sbuf("gt_t", [P, PACK], F32)
         windows = [sbuf(f"window{t}", [P, U], F32) for t in range(PACK)]
 
         nc.vector.memset(w1_raw[1][:].bitcast(I32), 0)
         for t in range(PACK):
-            engine = nc.vector if t < 2 else nc.gpsimd
-            engine.memset(windows[t][:], 0.0)
+            nc.vector.memset(windows[t][:].bitcast(I32), 0)
 
         nc.sync.dma_start(offs_t[:], offs)
         load_scales_everywhere(nc.sync, x_s, x_scales)
@@ -111,9 +109,8 @@ def tile_picked_candpage_sigmoid_po_kernel(
         nc.sync.dma_start(out=x_w[:].bitcast(I32), in_=as_words(x_words))
         nc.sync.dma_start(out=w1_raw[0][:].bitcast(I32), in_=as_words(w1_words))
         load_scales(nc.sync, w1_raw[1], w1_scales)
+        nc.sync.dma_start(out=gs_t[:], in_=gs.rearrange("(p t) o -> p (t o)", t=PACK))
         nc.sync.dma_start(slot_t[:], slot)
-        nc.gpsimd.dma_start(out=gs_t[:], in_=gs.rearrange("(p t) o -> p (t o)", t=PACK))
-        nc.gpsimd.dma_start(out=gt_t[:], in_=gt.rearrange("(p t) o -> p (t o)", t=PACK))
 
         xq_s = sbuf("xq_s", [P, S], U8)
         xc_s = sbuf("xc_s", [P, V], U8)
@@ -178,6 +175,8 @@ def tile_picked_candpage_sigmoid_po_kernel(
         for t in range(PACK):
             score_and_scatter(t, first, rest)
 
+        gt_t = sbuf("gs_t", [P, PACK], F32)
+        nc.sync.dma_start(out=gt_t[:], in_=gt.rearrange("(p t) o -> p (t o)", t=PACK))
         w2 = (sbuf("w1_raw_s", [P, N], U32), sbuf("z_grouped_first", [P, N], U8))
         w2_raw = (w2_raw_w, w2_raw_s)
         nc.vector.tensor_copy(out=dealt(w2[1]), in_=in_fours(w2_raw[1]))

@@ -16,7 +16,7 @@ PACK = 4
 K, T, S, V, N, U, H = 512, 2048, 512, 512, 512, 1024, 512
 FLOPS = 2 * K * H * S + 2 * K * V * S + 2 * V * N * U
 
-PLACE_SLICES = (128, 384)
+PLACE_SLICES = (256, 256)
 Z2_CHUNKS = (128, 256, 256, 384)
 SLOT_CHUNKS = (128, 256, 256, 256, 128)
 WORD_STORE_ENDS = (384, 896, 1024)
@@ -101,7 +101,7 @@ def tile_picked_candpage_sigmoid_po_kernel(
 
         nc.vector.memset(w1_raw[1][:].bitcast(I32), 0)
         for t in range(PACK):
-            nc.vector.memset(windows[t][:].bitcast(I32), 0)
+            (nc.vector if t < 2 else nc.gpsimd).memset(windows[t][:].bitcast(I32), 0)
 
         nc.sync.dma_start(offs_t[:], offs)
         load_scales_everywhere(nc.sync, x_s, x_scales)
@@ -131,19 +131,30 @@ def tile_picked_candpage_sigmoid_po_kernel(
             nc.vector.tensor_copy(out=words[:], in_=x_w[:].indirect(offs_t[:, j0 // 16 : (j0 + n) // 16]))
             return words
 
-        def project(j0, n, words):
+        def project_on_vector(j0, words, name):
+            h = bank([P, PACK, P])
+            for t in range(PACK):
+                mx(h[:, t, :], w1, slice(P * t, P * t + P), (words, xq_s), slice(j0, j0 + P))
+            grouped = sbuf(name, [P, PACK * P], BF16)
+            nc.vector.tensor_tensor(
+                out=grouped[:].rearrange("p (n t) -> p n t", t=PACK),
+                in0=h[:].rearrange("p t n -> p n t"),
+                in1=gs_t[:].unsqueeze(1).to_broadcast([P, P, PACK]),
+                op=mybir.AluOpType.mult,
+            )
+            return grouped
+
+        def project_on_scalar(j0, n, words, name):
             pairs = sbuf(f"z_pairs{j0}", [P, PACK * n], BF16)
             for t in range(PACK):
                 h = bank([P, n])
-                for a, width in pieces(0, n):
-                    cols = slice(a, a + width)
-                    mx(h[:, cols], w1, slice(P * t, P * t + P), (words, xq_s[:, j0 : j0 + n]), cols)
+                mx(h[:], w1, slice(P * t, P * t + P), (words, xq_s[:, j0 : j0 + n]), slice(0, n))
                 nc.scalar.activation(out=pair_slot(pairs, t), in_=h[:], func=ACT.Copy, scale=gs_t[:, t : t + 1])
-            return pairs
-
-        def join_z(n, pairs, name):
             grouped = sbuf(name, [P, PACK * n], BF16)
-            join_pairs(nc, grouped, pairs)
+            nc.scalar.copy(
+                out=grouped[:].bitcast(U32).rearrange("p (n u) -> p n u", u=2),
+                in_=pairs[:].bitcast(U32).rearrange("p (u n) -> p n u", u=2),
+            )
             return grouped
 
         def quantise_z(j0, n, grouped):
@@ -160,30 +171,32 @@ def tile_picked_candpage_sigmoid_po_kernel(
 
         first, rest = PLACE_SLICES
         words_first = gather_places(0, first, "xq_first")
-        words_rest = gather_places(first, rest, "w1_raw_s")
-        pairs_first = project(0, first, words_first)
-        xc = (sbuf("xq_first", [P, V], U32), xc_s)
+        xc = (sbuf("w1_raw_s", [P, V], U32), xc_s)
         nc.vector.tensor_copy(out=dealt(xc[0]), in_=x_w[:].indirect(cand_t[:]))
-        quantise_z(0, first, join_z(first, pairs_first, "z_grouped_first"))
+        grouped = [project_on_vector(0, words_first, "z_grouped0"), project_on_vector(P, words_first, "z_grouped_first")]
+        quantise_z(0, P, grouped[0])
+        quantise_z(P, P, grouped[1])
+        words_rest = gather_places(first, rest, "z_grouped_first")
         w2_raw_w = sbuf("w_raw_w", [P, N], U32)
         nc.sync.dma_start(out=w2_raw_w[:].bitcast(I32), in_=as_words(w2_words))
-        score_and_scatter(0, 0, first)
-        quantise_z(first, rest, join_z(rest, project(first, rest, words_rest), "z_grouped_rest"))
-        score_and_scatter(1, 0, first, f"z_pairs{first}")
-        score_and_scatter(2, 0, first)
-        score_and_scatter(3, 0, first, "z_grouped_rest")
-        for t in range(PACK):
+        score_and_scatter(0, 0, P)
+        score_and_scatter(0, P, P)
+        score_and_scatter(1, 0, first)
+        quantise_z(first, rest, project_on_scalar(first, rest, words_rest, "z_grouped_rest"))
+        score_and_scatter(2, 0, first, f"z_pairs{first}")
+        for t in range(PACK - 1):
             score_and_scatter(t, first, rest)
+        score_and_scatter(PACK - 1, 0, S)
 
         gt_t = sbuf("gs_t", [P, PACK], F32)
         nc.sync.dma_start(out=gt_t[:], in_=gt.rearrange("(p t) o -> p (t o)", t=PACK))
-        w2 = (sbuf("w1_raw_s", [P, N], U32), sbuf("z_grouped_first", [P, N], U8))
+        w2 = (sbuf("z_grouped_first", [P, N], U32), sbuf("scores3_0", [P, N], U8))
         w2_raw = (w2_raw_w, w2_raw_s)
         nc.vector.tensor_copy(out=dealt(w2[1]), in_=in_fours(w2_raw[1]))
 
         chunks = []
         w0 = 0
-        for width, host in zip(Z2_CHUNKS, ("xq_first", "xc_s", "z_w", "z_s")):
+        for width, host in zip(Z2_CHUNKS, ("w1_raw_s", "xc_s", "z_w", "z_s")):
             chunks.append((w0, width, sbuf(host, [P, PACK * width], BF16)))
             w0 += width
 

from contextlib import ExitStack

import concourse.mybir as mybir

F32 = mybir.dt.float32
BF16 = mybir.dt.bfloat16
I32 = mybir.dt.int32
U32 = mybir.dt.uint32
U16 = mybir.dt.uint16
U8 = mybir.dt.uint8
FP8X4 = mybir.dt.float8_e4m3fn_x4
ACT = mybir.ActivationFunctionType

P = 128
PACK = 4
K, T, S, V, N, U, H = 512, 2048, 512, 512, 512, 1024, 512
FLOPS = 2 * K * H * S + 2 * K * V * S + 2 * V * N * U

PLACE_SLICES = (256, 256)
Z2_CHUNKS = (128, 256, 256, 384)
SLOT_CHUNKS = (128, 256, 256, 256, 128)
WORD_STORE_ENDS = (384, 896, 1024)


def pieces(start, width):
    out = []
    while width > 0:
        n = 512 if width >= 512 else (256 if width >= 256 else 128)
        out.append((start, n))
        start, width = start + n, width - n
    return out


def as_words(packed):
    return packed[0].rearrange("p n t -> p (n t)").bitcast(I32)


def load_scales(queue, plane, scales):
    for q in range(4):
        queue.dma_start(out=plane[32 * q : 32 * q + 4, :].bitcast(I32), in_=scales[0, 4 * q : 4 * q + 4, :].bitcast(I32))


def load_scales_everywhere(queue, plane, scales):
    for q in range(4):
        rows = scales[0, 4 * q : 4 * q + 4, :].bitcast(I32).partition_broadcast(8)
        queue.dma_start(out=plane[32 * q : 32 * q + 32, :].bitcast(I32), in_=rows)


def dealt(tile):
    return tile[:].rearrange("p (t m) -> p m t", t=PACK)


def in_fours(tile):
    return tile[:].rearrange("p (m t) -> p m t", t=PACK)


def join_pairs(nc, grouped, pairs):
    nc.vector.tensor_copy(
        out=grouped[:].bitcast(I32).rearrange("p (n u) -> p n u", u=2),
        in_=pairs[:].bitcast(I32).rearrange("p (u n) -> p n u", u=2),
    )


def pair_slot(pairs, t):
    return pairs[:].rearrange("p (u n e) -> p u n e", u=2, e=2)[:, t // 2, :, t % 2]


def tile_picked_candpage_sigmoid_po_kernel(
    tc, x_words, x_scales, w1_words, w1_scales, gs, gt, w2_words, w2_scales, offs, cand, slot, out_0, out_1, out_2
):
    nc = tc.nc
    with ExitStack() as ctx:
        keep = ctx.enter_context(tc.tile_pool(name="keep", bufs=1))
        psum = ctx.enter_context(tc.psum_pool(name="psum", bufs=8))

        def sbuf(name, shape, dtype):
            return keep.tile(shape, dtype, name=name, align_bytes=64)

        def bank(shape):
            return psum.tile(shape, F32, name="bank")

        def mx(out, lhs, lhs_cols, rhs, rhs_cols):
            nc.tensor.matmul_mx(
                out=out,
                lhsT=lhs[0][:, lhs_cols].bitcast(FP8X4),
                lhsT_scale=lhs[1][:, lhs_cols],
                rhs=rhs[0][:, rhs_cols].bitcast(FP8X4),
                rhs_scale=rhs[1][:, rhs_cols],
                start=True,
                stop=True,
            )

        offs_t = keep.tile([P, S // 16], U16, name="offs_t")
        cand_t = keep.tile([P, V // 16], U16, name="cand_t")
        slot_t = keep.tile([P, S // 16], U16, name="slot_t")
        x_w = sbuf("x_w", [P, T], U32)
        x_s = sbuf("x_s", [P, T], U8)
        w1_raw = (sbuf("w_raw_w", [P, H], U32), sbuf("w1_raw_s", [P, H], U8))
        gs_t = sbuf("gs_t", [P, PACK], F32)
        windows = [sbuf(f"window{t}", [P, U], F32) for t in range(PACK)]

        nc.vector.memset(w1_raw[1][:].bitcast(I32), 0)
        for t in range(PACK):
            (nc.vector if t < 2 else nc.gpsimd).memset(windows[t][:].bitcast(I32), 0)

        nc.sync.dma_start(offs_t[:], offs)
        load_scales_everywhere(nc.sync, x_s, x_scales)
        nc.sync.dma_start(cand_t[:], cand)
        nc.sync.dma_start(out=x_w[:].bitcast(I32), in_=as_words(x_words))
        nc.sync.dma_start(out=w1_raw[0][:].bitcast(I32), in_=as_words(w1_words))
        load_scales(nc.sync, w1_raw[1], w1_scales)
        nc.sync.dma_start(out=gs_t[:], in_=gs.rearrange("(p t) o -> p (t o)", t=PACK))
        nc.sync.dma_start(slot_t[:], slot)

        xq_s = sbuf("xq_s", [P, S], U8)
        xc_s = sbuf("xc_s", [P, V], U8)
        w1 = (sbuf("w1_w", [P, H], U32), sbuf("w1_s", [P, H], U8))
        zq = (sbuf("z_w", [P, S], U32), sbuf("z_s", [P, S], U8))

        nc.vector.tensor_copy(out=xq_s[:], in_=x_s[:].indirect(offs_t[:]))
        nc.vector.tensor_copy(out=dealt(xc_s), in_=x_s[:].indirect(cand_t[:]))
        nc.scalar.copy(out=dealt(w1[0]), in_=in_fours(w1_raw[0]))
        nc.vector.tensor_copy(out=dealt(w1[1]), in_=in_fours(w1_raw[1]))

        w2_raw_s = sbuf("x_s", [P, N], U8)
        nc.vector.memset(w2_raw_s[:].bitcast(I32), 0)
        load_scales(nc.sync, w2_raw_s, w2_scales)

        def gather_places(j0, n, name):
            words = sbuf(name, [P, n], U32)
            nc.vector.tensor_copy(out=words[:], in_=x_w[:].indirect(offs_t[:, j0 // 16 : (j0 + n) // 16]))
            return words

        def project_on_vector(j0, words, name):
            h = bank([P, PACK, P])
            for t in range(PACK):
                mx(h[:, t, :], w1, slice(P * t, P * t + P), (words, xq_s), slice(j0, j0 + P))
            grouped = sbuf(name, [P, PACK * P], BF16)
            nc.vector.tensor_tensor(
                out=grouped[:].rearrange("p (n t) -> p n t", t=PACK),
                in0=h[:].rearrange("p t n -> p n t"),
                in1=gs_t[:].unsqueeze(1).to_broadcast([P, P, PACK]),
                op=mybir.AluOpType.mult,
            )
            return grouped

        def project_on_scalar(j0, n, words, name):
            pairs = sbuf(f"z_pairs{j0}", [P, PACK * n], BF16)
            for t in range(PACK):
                h = bank([P, n])
                mx(h[:], w1, slice(P * t, P * t + P), (words, xq_s[:, j0 : j0 + n]), slice(0, n))
                nc.scalar.activation(out=pair_slot(pairs, t), in_=h[:], func=ACT.Copy, scale=gs_t[:, t : t + 1])
            grouped = sbuf(name, [P, PACK * n], BF16)
            nc.scalar.copy(
                out=grouped[:].bitcast(U32).rearrange("p (n u) -> p n u", u=2),
                in_=pairs[:].bitcast(U32).rearrange("p (u n) -> p n u", u=2),
            )
            return grouped

        def quantise_z(j0, n, grouped):
            nc.vector.quantize_mx(out=zq[0][:, j0 : j0 + n].bitcast(FP8X4), scales=zq[1][:, j0 : j0 + n], in_=grouped[:])

        def score_and_scatter(t, j0, n, name=None):
            logits = bank([P, n])
            for a, width in pieces(0, n):
                mx(logits[:, a : a + width], xc, slice(P * t, P * t + P), zq, slice(j0 + a, j0 + a + width))
            scores = sbuf(name or f"scores{t}_{j0}", [P, n], F32)
            nc.scalar.activation(out=scores[:], in_=logits[:], func=ACT.Sigmoid, scale=0.0625)
            target = windows[t][:].indirect(slot_t[:, j0 // 16 : (j0 + n) // 16])
            nc.vector.tensor_copy(out=target, in_=scores[:])

        first, rest = PLACE_SLICES
        words_first = gather_places(0, first, "xq_first")
        xc = (sbuf("w1_raw_s", [P, V], U32), xc_s)
        nc.vector.tensor_copy(out=dealt(xc[0]), in_=x_w[:].indirect(cand_t[:]))
        grouped = [project_on_vector(0, words_first, "z_grouped0"), project_on_vector(P, words_first, "z_grouped_first")]
        quantise_z(0, P, grouped[0])
        quantise_z(P, P, grouped[1])
        words_rest = gather_places(first, rest, "z_grouped_first")
        w2_raw_w = sbuf("w_raw_w", [P, N], U32)
        nc.sync.dma_start(out=w2_raw_w[:].bitcast(I32), in_=as_words(w2_words))
        score_and_scatter(0, 0, P)
        score_and_scatter(0, P, P)
        score_and_scatter(1, 0, first)
        quantise_z(first, rest, project_on_scalar(first, rest, words_rest, "z_grouped_rest"))
        score_and_scatter(2, 0, first, f"z_pairs{first}")
        for t in range(PACK - 1):
            score_and_scatter(t, first, rest)
        score_and_scatter(PACK - 1, 0, S)

        gt_t = sbuf("gs_t", [P, PACK], F32)
        nc.sync.dma_start(out=gt_t[:], in_=gt.rearrange("(p t) o -> p (t o)", t=PACK))
        w2 = (sbuf("z_grouped_first", [P, N], U32), sbuf("scores3_0", [P, N], U8))
        w2_raw = (w2_raw_w, w2_raw_s)
        nc.vector.tensor_copy(out=dealt(w2[1]), in_=in_fours(w2_raw[1]))

        chunks = []
        w0 = 0
        for width, host in zip(Z2_CHUNKS, ("w1_raw_s", "xc_s", "z_w", "z_s")):
            chunks.append((w0, width, sbuf(host, [P, PACK * width], BF16)))
            w0 += width

        def weigh(t, chunk):
            w0, width, pairs = chunk
            nc.scalar.activation(
                out=pair_slot(pairs, t), in_=windows[t][:, w0 : w0 + width], func=ACT.Copy, scale=gt_t[:, t : t + 1]
            )

        nc.scalar.copy(out=dealt(w2[0]), in_=in_fours(w2_raw[0]))
        for t in range(PACK):
            for chunk in chunks:
                weigh(t, chunk)

        z2q = (sbuf("z2_w", [P, U], U32), sbuf("z2_s", [P, U], U8))
        yq = (sbuf("y_w", [P, U], U32), sbuf("y_s", [P, U], U8))
        out_rows = out_0.rearrange("(p t) w -> p t w", t=PACK)
        out_words = as_words(out_1)
        stored = 0
        for w0, width, pairs in chunks:
            cols = slice(w0, w0 + width)
            grouped = sbuf(f"z2_grouped{w0}", [P, PACK * width], BF16)
            join_pairs(nc, grouped, pairs)
            nc.vector.quantize_mx(out=z2q[0][:, cols].bitcast(FP8X4), scales=z2q[1][:, cols], in_=grouped[:])
        for w0, width in zip([sum(SLOT_CHUNKS[:i]) for i in range(len(SLOT_CHUNKS))], SLOT_CHUNKS):
            cols = slice(w0, w0 + width)
            y = sbuf(f"y{w0}", [P, PACK, width], F32)
            per_bank = 512 // width
            for t0 in range(0, PACK, per_bank):
                acc = bank([P, per_bank, width])
                for i in range(per_bank):
                    t = t0 + i
                    mx(acc[:, i, :], w2, slice(P * t, P * t + P), z2q, cols)
                nc.scalar.copy(out=y[:, t0 : t0 + per_bank, :], in_=acc[:])
            nc.sync.dma_start(out=out_rows[:, :, cols], in_=y[:])
            y_grouped = sbuf(f"y_grouped{w0}", [P, PACK * width], BF16)
            nc.vector.tensor_copy(
                out=y_grouped[:].rearrange("p (c i t) -> p c t i", i=4, t=PACK),
                in_=y[:].rearrange("p t (c i) -> p c t i", i=4),
            )
            nc.vector.quantize_mx(out=yq[0][:, cols].bitcast(FP8X4), scales=yq[1][:, cols], in_=y_grouped[:])
            if w0 + width in WORD_STORE_ENDS:
                nc.sync.dma_start(out=out_words[:, stored : w0 + width], in_=yq[0][:, stored : w0 + width].bitcast(I32))
                stored = w0 + width
        for q in range(4):
            queue = nc.sync if q % 2 == 0 else nc.scalar
            queue.dma_start(out=out_2[0, 4 * q : 4 * q + 4, :].bitcast(I32), in_=yq[1][32 * q : 32 * q + 4, :].bitcast(I32))
